import numpy as np
import ml_dtypes


def mxq(x, axis, fmt="e4m3"):
    dtype, down = {"e4m3": (ml_dtypes.float8_e4m3fn, 7), "e5m2": (ml_dtypes.float8_e5m2, 14)}[fmt]
    v = np.moveaxis(np.asarray(x, np.float32).astype(ml_dtypes.bfloat16).astype(np.float64), axis, -1)
    blocks = v.reshape(v.shape[:-1] + (-1, 32))
    amax = np.abs(blocks).max(-1, keepdims=True)
    byte = np.maximum(np.where(amax > 0, np.frexp(amax)[1] - 1 + 127, 0) - down, 1)
    scale = np.exp2(byte - 127.0)
    codes = (blocks / scale).astype(np.float32).astype(dtype).astype(np.float64)
    return np.moveaxis((codes * scale).reshape(v.shape), -1, axis)


WIDE = False


def mx_kscale(k):
    if not WIDE:
        return np.ones(k)
    levels = np.array([10, -10, 5, -5, 0])
    if k % 512:
        return np.exp2(np.random.permutation(np.resize(levels, k // 32))).repeat(32)
    a = np.empty((k // 512, 16))
    for p in range(k // 512):
        a[p, :8] = np.random.permutation(np.resize(levels, 8))
        for g in range(8):
            far = levels[np.abs(levels - a[p, g]) >= 10]
            a[p, g + 8] = far[np.random.randint(len(far))]
    return np.exp2(a.ravel()).repeat(32)


BF16 = ml_dtypes.bfloat16


def bf(x):
    return np.asarray(x, np.float32).astype(BF16)


def f64(x):
    return np.asarray(x).astype(np.float64)


E2M1 = np.array([0.0, 0.5, 1.0, 1.5, 2.0, 3.0, 4.0, 6.0, -0.0, -0.5, -1.0, -1.5, -2.0, -3.0, -4.0, -6.0])


def pack_weight(w, fmt):
    k, n = w.shape
    w = f64(bf(w)).reshape(k // 32, 32, n)
    amax = np.abs(w).max(1)
    if fmt == "e4m3":
        byte = np.frexp(amax)[1] - 1 + 127 - 7
    else:
        mant, ex = np.frexp(amax / 6.0)
        byte = np.where(mant > 0.5, ex, ex - 1) + 127
    byte = np.clip(np.where(amax > 0, byte, 1), 1, 254)
    scaled = (w * np.exp2(127.0 - byte)[:, None, :]).reshape(k, n).astype(np.float32)
    by_word = np.ascontiguousarray(scaled.reshape(k // 512, 128, 4, n).transpose(0, 1, 3, 2))
    if fmt == "e4m3":
        words = by_word.astype(ml_dtypes.float8_e4m3fn).view(np.uint8)
    else:
        c = by_word.astype(ml_dtypes.float4_e2m1fn).view(np.uint8) & 0xF
        words = c[..., 0::2] | (c[..., 1::2] << 4)
    return np.ascontiguousarray(words), np.ascontiguousarray(byte.astype(np.uint8).reshape(k // 512, 16, n))


def unpack_weight(words, scales, fmt):
    g, p, n, _ = words.shape
    if fmt == "e4m3":
        vals = np.ascontiguousarray(words).view(ml_dtypes.float8_e4m3fn).astype(np.float64)
    else:
        nib = np.empty((g, p, n, 4), np.uint8)
        nib[..., 0::2] = words & 0xF
        nib[..., 1::2] = words >> 4
        vals = E2M1[nib]
    vals = vals * np.repeat(np.exp2(scales.astype(np.float64) - 127.0), 8, axis=1)[..., None]
    return vals.transpose(0, 1, 3, 2).reshape(g * 512, n)
def pack4(w):
    words, scales = pack_weight(w, "e2m1")
    return words.reshape(words.shape[0], 128, -1), scales


def unpack4(words, scales):
    return unpack_weight(words.reshape(words.shape[0], 128, -1, 2), scales, "e2m1")


M, KA, KB, N, B = 2048, 512, 1024, 1024, 512

VOL_A, VOL_B = 0.4, 0.3


def setup_inputs():
    s = mx_kscale(KA)
    u = mx_kscale(KB)
    t = mx_kscale(N)
    lb = np.random.standard_normal((KB, N)) * VOL_B / np.sqrt(KB) / u[:, None]
    w = np.random.standard_normal((N, B)) / np.sqrt(N) / t[:, None]
    lb_words, lb_scales = pack4(lb)
    w_words, w_scales = pack4(w)
    return {"za": bf(np.random.standard_normal((M, KA)) * s),
            "zb": bf(np.random.standard_normal((M, KB)) * u),
            "la": bf(np.random.standard_normal((KA, N)) * VOL_A / np.sqrt(KA) / s[:, None]),
            "lb_words": lb_words,
            "lb_scales": lb_scales,
            "forward": bf((1 + 0.1 * np.random.standard_normal(N)) * t),
            "w_words": w_words,
            "w_scales": w_scales,
            "strike": bf(0.3 * np.random.standard_normal(B))}


def reference(za, zb, la, lb_words, lb_scales, forward, w_words, w_scales, strike):
    main = mxq(f64(za), 1, "e4m3") @ mxq(f64(la), 0, "e4m3")
    minor = mxq(f64(zb), 1, "e4m3") @ unpack4(lb_words, lb_scales)
    price = np.exp(main + minor) * f64(forward)
    basket = mxq(price, 1, "e4m3") @ unpack4(w_words, w_scales)
    return np.maximum(basket - f64(strike), 0.0)

@@ -1,0 +1,334 @@
+from contextlib import ExitStack
+
+import concourse.mybir as mybir
+from concourse.masks import make_identity
+
+M, KA, KB, N, B = 2048, 512, 1024, 1024, 512
+FLOPS = 2 * M * (KA + KB) * N + 2 * M * N * B
+
+F32 = mybir.dt.float32
+BF16 = mybir.dt.bfloat16
+U32 = mybir.dt.uint32
+I32 = mybir.dt.int32
+U8 = mybir.dt.uint8
+FP8X4 = mybir.dt.float8_e4m3fn_x4
+FP4X4 = mybir.dt.float4_e2m1fn_x4
+ACT = mybir.ActivationFunctionType
+ALU = mybir.AluOpType
+
+P = 128
+PACK = 4
+KP = 512
+TILE = 512
+TILES = M // TILE
+PASSES = 3
+
+
+def tile_basket_option_payoff_s3_kernel(tc, za, zb, la, lb_words, lb_scales, forward, w_words, w_scales, strike, out):
+    nc = tc.nc
+    with ExitStack() as ctx:
+        keep = ctx.enter_context(tc.tile_pool(name="keep", bufs=1))
+        work = ctx.enter_context(tc.tile_pool(name="work", bufs=2))
+        psum = ctx.enter_context(tc.psum_pool(name="psum", bufs=8))
+        ctx.enter_context(tc.manual_schedule())
+
+        def kept(name, shape, dtype):
+            return keep.tile(shape, dtype, name=name, align_bytes=64)
+
+        def bank():
+            return psum.tile([P, 512], F32, name="bank")
+
+        ident = kept("ident", [P, P], F32)
+        make_identity(nc, ident[:])
+
+        lbs_raw = kept("lbs_raw", [P, 2, N], U8)
+        ws = kept("ws", [P, 2, B], U8)
+        nc.vector.memset(lbs_raw[:].bitcast(I32), 0)
+        nc.vector.memset(ws[:].bitcast(I32), 0)
+
+        def load_scales(plane, src):
+            for q in range(4):
+                nc.sync.dma_start(
+                    out=plane[32 * q : 32 * q + 4, :, :].bitcast(I32),
+                    in_=src[:, 4 * q : 4 * q + 4, :].rearrange("g r n -> r g n").bitcast(I32),
+                )
+
+        z_raw = {}
+
+        def load_z(mt, c):
+            src = zb[:, KP * c : KP * (c + 1)] if c < 2 else za
+            t = kept("z_raw_%d_%d" % (mt, c), [P, PACK, KP], BF16)
+            nc.sync.dma_start(out=t[:], in_=src[TILE * mt : TILE * (mt + 1), :].rearrange("(p j) k -> p j k", j=PACK))
+            z_raw[mt, c] = t
+
+        lb_raw = {}
+
+        def load_lb(c, g):
+            t = kept("lb_raw_%d_%d" % (c, g), [P, 2 * KP], U8)
+            nc.sync.dma_start(out=t[:].bitcast(I32), in_=lb_words[c, :, 2 * KP * g : 2 * KP * (g + 1)].bitcast(I32))
+            lb_raw[c, g] = t
+
+        la_raw = {}
+
+        def load_la(g):
+            t = kept("la_raw_%d" % g, [P, PACK, KP], BF16)
+            nc.sync.dma_start(out=t[:], in_=la[:, KP * g : KP * (g + 1)].rearrange("(p j) n -> p j n", j=PACK))
+            la_raw[g] = t
+
+        load_z(0, 0)
+        load_lb(0, 0)
+        load_scales(lbs_raw, lb_scales)
+        load_z(0, 1)
+        load_lb(1, 0)
+        load_la(0)
+        load_z(0, 2)
+        load_lb(0, 1)
+        load_lb(1, 1)
+        load_la(1)
+        fwd = kept("fwd", [P, 2, PACK], BF16)
+        nc.sync.dma_start(out=fwd[:], in_=forward.rearrange("(g p t) -> p g t", p=P, t=PACK))
+        for c in range(PASSES):
+            load_z(1, c)
+        load_scales(ws, w_scales)
+        ww = kept("ww", [P, 2, 2 * B], U8)
+        nc.sync.dma_start(out=ww[:].bitcast(I32), in_=w_words.rearrange("g p n -> p g n").bitcast(I32))
+        strike_b = kept("strike_b", [P, B], BF16)
+        nc.sync.dma_start(out=strike_b[:], in_=strike.partition_broadcast(P))
+        for mt in range(2, TILES):
+            for c in range(PASSES):
+                load_z(mt, c)
+
+        w1_codes = {}
+        w1_scales = {}
+
+        def sort_lb_codes(c, g):
+            t = kept("lb_codes_%d_%d" % (c, g), [P, 2 * KP], U8)
+            nc.vector.tensor_copy(
+                out=t[:].rearrange("p (t a m b) -> p a t m b", t=PACK, m=8, b=2),
+                in_=lb_raw[c, g][:].rearrange("p (a m t b) -> p a t m b", t=PACK, m=8, b=2),
+            )
+            for s in range(PACK):
+                w1_codes[c, g, s] = t[:, 2 * P * s : 2 * P * (s + 1)].bitcast(FP4X4)
+
+        def sort_lb_scales(g):
+            t = kept("lb_scales_%d" % g, [P, 2, KP], U8)
+            nc.vector.tensor_copy(
+                out=t[:].rearrange("p c (t a m) -> p c a t m", t=PACK, m=16),
+                in_=lbs_raw[:, :, KP * g : KP * (g + 1)].rearrange("p c (a m t) -> p c a t m", t=PACK, m=16),
+            )
+            for c in range(2):
+                for s in range(PACK):
+                    w1_scales[c, g, s] = t[:, c, P * s : P * (s + 1)]
+
+        la_sorted = {}
+
+        def sort_la(g):
+            t = kept("la_sorted_%d" % g, [P, PACK * KP], BF16)
+            nc.vector.tensor_copy(
+                out=t[:].rearrange("p (t a m j) -> p a t m j", t=PACK, m=2, j=PACK),
+                in_=la_raw[g][:].rearrange("p j (a m t) -> p a t m j", t=PACK, m=2),
+            )
+            la_sorted[g] = t
+
+        def quant_la(g):
+            codes = kept("la_codes_%d" % g, [P, KP], U32)
+            scales = kept("la_scales_%d" % g, [P, KP], U8)
+            nc.vector.quantize_mx(out=codes[:].bitcast(FP8X4), scales=scales[:], in_=la_sorted[g][:])
+            for s in range(PACK):
+                w1_codes[2, g, s] = codes[:, P * s : P * (s + 1)].bitcast(FP8X4)
+                w1_scales[2, g, s] = scales[:, P * s : P * (s + 1)]
+
+        z_t = {}
+        z_codes = {}
+        z_scales = {}
+
+        def turn_z(mt, c, h):
+            if h == 0:
+                z_t[mt, c] = work.tile([P, PACK * TILE], BF16, name="z_t", bufs=3, align_bytes=64)
+            words = z_raw[mt, c][:].rearrange("p j k -> p (j k)").bitcast(F32)
+            ps = bank()
+            for jj in range(2):
+                j = 2 * h + jj
+                for u in range(2):
+                    nc.tensor.transpose(
+                        ps[:, P * (2 * jj + u) : P * (2 * jj + u + 1)],
+                        words[:, 256 * j + u : 256 * (j + 1) : 2],
+                        ident[:],
+                    )
+            nc.scalar.copy(
+                out=z_t[mt, c][:].bitcast(F32)[:, 512 * h : 512 * (h + 1)].rearrange("p (j r u) -> p j r u", j=2, u=2),
+                in_=ps[:].rearrange("p (j u r) -> p j r u", j=2, u=2),
+            )
+
+        def quant_z(mt, c):
+            z_codes[mt, c] = work.tile([P, TILE], U32, name="z_codes", bufs=6, align_bytes=64)
+            z_scales[mt, c] = work.tile([P, TILE], U8, name="z_scales", bufs=6, align_bytes=64)
+            nc.vector.quantize_mx(out=z_codes[mt, c][:].bitcast(FP8X4), scales=z_scales[mt, c][:], in_=z_t[mt, c][:])
+
+        def pass1(dst, mt, g, s, c, cols):
+            nc.tensor.matmul_mx(
+                out=dst,
+                lhsT=w1_codes[c, g, s],
+                lhsT_scale=w1_scales[c, g, s],
+                rhs=z_codes[mt, c][:, cols].bitcast(FP8X4),
+                rhs_scale=z_scales[mt, c][:, cols],
+                start=(c == 0),
+                stop=(c == PASSES - 1),
+            )
+
+        growth = {}
+
+        def exp_slot(ps, mt, g, s):
+            if s == 0:
+                growth[mt, g] = work.tile([P, PACK, TILE], F32, name="growth", bufs=2)
+            nc.scalar.activation(out=growth[mt, g][:, s, :], in_=ps[:], func=ACT.Exp)
+
+        def returns(mt, g, s):
+            ps = bank()
+            for c in range(PASSES):
+                pass1(ps[:], mt, g, s, c, slice(0, TILE))
+            exp_slot(ps, mt, g, s)
+
+        price = {}
+        p_codes = {}
+        p_scales = {}
+
+        def new_price(mt, g):
+            price[mt, g] = work.tile([P, PACK * TILE], BF16, name="price", bufs=2, align_bytes=64)
+            p_codes[mt, g] = work.tile([P, TILE], U32, name="p_codes", bufs=4, align_bytes=64)
+            p_scales[mt, g] = work.tile([P, TILE], U8, name="p_scales", bufs=4, align_bytes=64)
+
+        def scale_price(mt, g, h):
+            if h == 0:
+                new_price(mt, g)
+            half = TILE // 2
+            nc.vector.tensor_tensor(
+                out=price[mt, g][:, PACK * half * h : PACK * half * (h + 1)].rearrange("p (a i t) -> p a t i", i=4, t=PACK),
+                in0=growth[mt, g][:, :, half * h : half * (h + 1)].rearrange("p t (a i) -> p a t i", i=4),
+                in1=fwd[:, g, :].unsqueeze(1).unsqueeze(3).to_broadcast([P, half // 4, PACK, 4]),
+                op=ALU.mult,
+            )
+
+        def quant_price(mt, g, cols):
+            nc.vector.quantize_mx(
+                out=p_codes[mt, g][:, cols].bitcast(FP8X4),
+                scales=p_scales[mt, g][:, cols],
+                in_=price[mt, g][:, PACK * cols.start : PACK * cols.stop],
+            )
+
+        def quant_price_halves(mt, g):
+            for h in range(2):
+                quant_price(mt, g, slice(256 * h, 256 * (h + 1)))
+
+        def baskets(mt, j):
+            ps = bank()
+            cols = slice(P * j, P * (j + 1))
+            for g in range(2):
+                nc.tensor.matmul_mx(
+                    out=ps[:],
+                    lhsT=p_codes[mt, g][:, cols].bitcast(FP8X4),
+                    lhsT_scale=p_scales[mt, g][:, cols],
+                    rhs=ww[:, g, :].bitcast(FP4X4),
+                    rhs_scale=ws[:, g, :],
+                    start=(g == 0),
+                    stop=(g == 1),
+                )
+            gain = work.tile([P, B], F32, name="gain", bufs=3)
+            nc.vector.tensor_tensor(out=gain[:], in0=ps[:], in1=strike_b[:], op=ALU.subtract)
+            payoff = work.tile([P, B], F32, name="payoff", bufs=4)
+            nc.scalar.activation(out=payoff[:], in_=gain[:], func=ACT.Relu)
+            rows = out[TILE * mt : TILE * (mt + 1), :].rearrange("(p j) b -> p j b", j=PACK)
+            nc.sync.dma_start(out=rows[:, j, :], in_=payoff[:])
+
+        grown = {}
+
+        def narrow_returns(mt, g, j):
+            ps = bank()
+            cols = slice(P * j, P * (j + 1))
+            for s in range(PACK):
+                for c in range(PASSES):
+                    pass1(ps[:, P * s : P * (s + 1)], mt, g, s, c, cols)
+            grown[j] = work.tile([P, P, PACK], F32, name="grown", bufs=4)
+            nc.scalar.activation(out=grown[j][:], in_=ps[:].rearrange("p (t n) -> p n t", t=PACK), func=ACT.Exp)
+
+        def narrow_price(mt, g, j):
+            nc.vector.tensor_tensor(
+                out=price[mt, g][:, PACK * P * j : PACK * P * (j + 1)].rearrange("p (n t) -> p n t", t=PACK),
+                in0=grown[j][:],
+                in1=fwd[:, g, :].unsqueeze(1).to_broadcast([P, P, PACK]),
+                op=ALU.mult,
+            )
+
+        whole = slice(0, TILE)
+        sort_lb_codes(0, 0)
+        sort_lb_scales(0)
+        sort_lb_codes(1, 0)
+        for c in range(2):
+            for h in range(2):
+                turn_z(0, c, h)
+        quant_z(0, 0)
+        first = [bank() for s in range(PACK)]
+        for s in range(PACK):
+            pass1(first[s][:], 0, 0, s, 0, whole)
+        sort_la(0)
+        quant_z(0, 1)
+        quant_la(0)
+        for h in range(2):
+            turn_z(0, 2, h)
+        quant_z(0, 2)
+        for s in range(PACK):
+            pass1(first[s][:], 0, 0, s, 1, whole)
+        for s in range(PACK):
+            pass1(first[s][:], 0, 0, s, 2, whole)
+            exp_slot(first[s], 0, 0, s)
+        sort_lb_codes(0, 1)
+        sort_lb_scales(1)
+        sort_lb_codes(1, 1)
+        sort_la(1)
+        quant_la(1)
+
+        for mt in range(TILES - 1):
+            if mt > 0:
+                for s in range(PACK):
+                    returns(mt, 0, s)
+            for c, h in ((0, 0), (0, 1), (1, 0)):
+                turn_z(mt + 1, c, h)
+            scale_price(mt, 0, 0)
+            quant_z(mt + 1, 0)
+            if mt > 0:
+                for j in range(PACK):
+                    baskets(mt - 1, j)
+            else:
+                for s in range(2):
+                    returns(mt, 1, s)
+            scale_price(mt, 0, 1)
+            quant_price_halves(mt, 0)
+            for c, h in ((1, 1), (2, 0), (2, 1)):
+                turn_z(mt + 1, c, h)
+            quant_z(mt + 1, 1)
+            quant_z(mt + 1, 2)
+            for s in range(0 if mt > 0 else 2, PACK):
+                returns(mt, 1, s)
+            for h in range(2):
+                scale_price(mt, 1, h)
+            quant_price_halves(mt, 1)
+
+        mt = TILES - 1
+        for s in range(PACK):
+            returns(mt, 0, s)
+        narrow_returns(mt, 1, 0)
+        scale_price(mt, 0, 0)
+        for j in range(PACK):
+            baskets(mt - 1, j)
+        for j in range(1, PACK):
+            narrow_returns(mt, 1, j)
+        scale_price(mt, 0, 1)
+        quant_price_halves(mt, 0)
+        new_price(mt, 1)
+        for step in range(PACK + 2):
+            if step < PACK:
+                narrow_price(mt, 1, step)
+            if 1 <= step <= PACK:
+                quant_price(mt, 1, slice(P * (step - 1), P * step))
+            if step >= 2:
+                baskets(mt, step - 2)

@@ -17,14 +17,32 @@ ACT = mybir.ActivationFunctionType
 ALU = mybir.AluOpType
 
 P = 128
-PACK = 4
-KP = 512
+SLOTS = 4
+K_PASS = P * SLOTS
+PAIRS = K_PASS // 2
 TILE = 512
+QUARTERS = TILE // P
 TILES = M // TILE
-PASSES = 3
+PASSES = (KB + KA) // K_PASS
+ZA_PASS = PASSES - 1
+LINE = 4
+
+LA_BLOCKS_ON_SCALAR = 16
+FIRST_RUN_TILE_1 = 3
+FIRST_RUN = 4
+
+WHOLE = slice(0, TILE)
+HALVES = (slice(0, TILE // 2), slice(TILE // 2, TILE))
+QUARTER_COLS = tuple(slice(P * j, P * (j + 1)) for j in range(QUARTERS))
 
 
-def tile_basket_option_payoff_s3_kernel(tc, za, zb, la, lb_words, lb_scales, forward, w_words, w_scales, strike, out):
+def quarter(j):
+    return slice(P * j, P * (j + 1))
+
+
+def tile_basket_option_payoff_s3_kernel(
+    tc, za, zb, la, lb_words, lb_scales, forward, w_words, w_scales, strike, out
+):
     nc = tc.nc
     with ExitStack() as ctx:
         keep = ctx.enter_context(tc.tile_pool(name="keep", bufs=1))
@@ -36,299 +54,341 @@ def tile_basket_option_payoff_s3_kernel(tc, za, zb, la, lb_words, lb_scales, for
             return keep.tile(shape, dtype, name=name, align_bytes=64)
 
         def bank():
-            return psum.tile([P, 512], F32, name="bank")
+            return psum.tile([P, TILE], F32, name="bank")
+
+        def mx_tiles(name, bufs):
+            codes = work.tile([P, TILE], U32, name=name + "_codes", bufs=bufs, align_bytes=64)
+            scales = work.tile([P, TILE], U8, name=name + "_scales", bufs=bufs, align_bytes=64)
+            return codes, scales
 
         ident = kept("ident", [P, P], F32)
         make_identity(nc, ident[:])
 
-        lbs_raw = kept("lbs_raw", [P, 2, N], U8)
-        ws = kept("ws", [P, 2, B], U8)
-        nc.vector.memset(lbs_raw[:].bitcast(I32), 0)
-        nc.vector.memset(ws[:].bitcast(I32), 0)
+        lb_scales_raw = kept("lb_scales_raw", [P, 2, N], U8)
+        w_scales_sb = kept("w_scales_sb", [P, 2, B], U8)
+        nc.vector.memset(lb_scales_raw[:].bitcast(I32), 0)
+        nc.vector.memset(w_scales_sb[:].bitcast(I32), 0)
 
-        def load_scales(plane, src):
+        def load_scales(queue, dst, src):
             for q in range(4):
-                nc.sync.dma_start(
-                    out=plane[32 * q : 32 * q + 4, :, :].bitcast(I32),
-                    in_=src[:, 4 * q : 4 * q + 4, :].rearrange("g r n -> r g n").bitcast(I32),
+                queue.dma_start(
+                    out=dst[32 * q : 32 * q + 4, :, :].bitcast(I32),
+                    in_=src[:, 4 * q : 4 * q + 4, :].rearrange("c r n -> r c n").bitcast(I32),
                 )
 
-        z_raw = {}
+        turn_src = {}
+        zb_words = {}
 
-        def load_z(mt, c):
-            src = zb[:, KP * c : KP * (c + 1)] if c < 2 else za
-            t = kept("z_raw_%d_%d" % (mt, c), [P, PACK, KP], BF16)
-            nc.sync.dma_start(out=t[:], in_=src[TILE * mt : TILE * (mt + 1), :].rearrange("(p j) k -> p j k", j=PACK))
-            z_raw[mt, c] = t
+        def load_z(mt, src, passes, part, parts):
+            width = src.shape[1]
+            rows = src[TILE * mt : TILE * (mt + 1), :].rearrange("(p j) k -> p j k", j=QUARTERS)
+            count = QUARTERS // parts
+            raw = kept("z_raw_%d_%d_%d" % (mt, passes[0], part), [P, count, width], BF16)
+            nc.sync.dma_start(out=raw[:], in_=rows[:, count * part : count * (part + 1), :])
+            words = raw[:].rearrange("p j k -> p (j k)").bitcast(F32)
+            for j in range(count):
+                for i, c in enumerate(passes):
+                    at = (width // 2) * j + PAIRS * i
+                    for u in range(2):
+                        turn_src[mt, c, count * part + j, u] = words[:, at + u : at + PAIRS : 2]
+            return words
 
         lb_raw = {}
 
         def load_lb(c, g):
-            t = kept("lb_raw_%d_%d" % (c, g), [P, 2 * KP], U8)
-            nc.sync.dma_start(out=t[:].bitcast(I32), in_=lb_words[c, :, 2 * KP * g : 2 * KP * (g + 1)].bitcast(I32))
-            lb_raw[c, g] = t
+            lb_raw[c, g] = kept("lb_raw_%d_%d" % (c, g), [P, 2 * K_PASS], U8)
+            src = lb_words[c, :, 2 * K_PASS * g : 2 * K_PASS * (g + 1)]
+            nc.sync.dma_start(out=lb_raw[c, g][:].bitcast(I32), in_=src.bitcast(I32))
 
         la_raw = {}
 
         def load_la(g):
-            t = kept("la_raw_%d" % g, [P, PACK, KP], BF16)
-            nc.sync.dma_start(out=t[:], in_=la[:, KP * g : KP * (g + 1)].rearrange("(p j) n -> p j n", j=PACK))
-            la_raw[g] = t
+            la_raw[g] = kept("la_raw_%d" % g, [P, SLOTS, K_PASS], BF16)
+            src = la[:, K_PASS * g : K_PASS * (g + 1)].rearrange("(p t) n -> p t n", t=SLOTS)
+            nc.sync.dma_start(out=la_raw[g][:], in_=src)
 
-        load_z(0, 0)
+        zb_passes = (0, 1)
+        load_z(0, zb, zb_passes, 0, 2)
         load_lb(0, 0)
-        load_scales(lbs_raw, lb_scales)
-        load_z(0, 1)
+        load_scales(nc.scalar, lb_scales_raw, lb_scales)
+        load_z(0, zb, zb_passes, 1, 2)
         load_lb(1, 0)
+        load_z(0, za, (ZA_PASS,), 0, 1)
         load_la(0)
-        load_z(0, 2)
         load_lb(0, 1)
         load_lb(1, 1)
         load_la(1)
-        fwd = kept("fwd", [P, 2, PACK], BF16)
-        nc.sync.dma_start(out=fwd[:], in_=forward.rearrange("(g p t) -> p g t", p=P, t=PACK))
-        for c in range(PASSES):
-            load_z(1, c)
-        load_scales(ws, w_scales)
-        ww = kept("ww", [P, 2, 2 * B], U8)
-        nc.sync.dma_start(out=ww[:].bitcast(I32), in_=w_words.rearrange("g p n -> p g n").bitcast(I32))
-        strike_b = kept("strike_b", [P, B], BF16)
-        nc.sync.dma_start(out=strike_b[:], in_=strike.partition_broadcast(P))
+        fwd = kept("fwd", [P, 2, SLOTS], BF16)
+        nc.sync.dma_start(out=fwd[:], in_=forward.rearrange("(g p t) -> p g t", p=P, t=SLOTS))
+        for part in range(2):
+            load_z(1, zb, zb_passes, part, 2)
+        load_z(1, za, (ZA_PASS,), 0, 1)
+        load_scales(nc.sync, w_scales_sb, w_scales)
+        w_codes = kept("w_codes", [P, 2, 2 * B], U8)
+        nc.sync.dma_start(out=w_codes[:].bitcast(I32), in_=w_words.rearrange("g p n -> p g n").bitcast(I32))
+        strike_rows = kept("strike_rows", [P, B], BF16)
+        nc.sync.dma_start(out=strike_rows[:], in_=strike.partition_broadcast(P))
         for mt in range(2, TILES):
-            for c in range(PASSES):
-                load_z(mt, c)
+            zb_words[mt] = load_z(mt, zb, zb_passes, 0, 1)
+            load_z(mt, za, (ZA_PASS,), 0, 1)
 
-        w1_codes = {}
-        w1_scales = {}
+        weight_codes = {}
+        weight_scales = {}
 
         def sort_lb_codes(c, g):
-            t = kept("lb_codes_%d_%d" % (c, g), [P, 2 * KP], U8)
+            codes = kept("lb_codes_%d_%d" % (c, g), [P, 2 * K_PASS], U8)
             nc.vector.tensor_copy(
-                out=t[:].rearrange("p (t a m b) -> p a t m b", t=PACK, m=8, b=2),
-                in_=lb_raw[c, g][:].rearrange("p (a m t b) -> p a t m b", t=PACK, m=8, b=2),
+                out=codes[:].rearrange("p (t a m b) -> p a t m b", t=SLOTS, m=8, b=2),
+                in_=lb_raw[c, g][:].rearrange("p (a m t b) -> p a t m b", t=SLOTS, m=8, b=2),
             )
-            for s in range(PACK):
-                w1_codes[c, g, s] = t[:, 2 * P * s : 2 * P * (s + 1)].bitcast(FP4X4)
+            for t in range(SLOTS):
+                weight_codes[c, g, t] = codes[:, 2 * P * t : 2 * P * (t + 1)].bitcast(FP4X4)
 
         def sort_lb_scales(g):
-            t = kept("lb_scales_%d" % g, [P, 2, KP], U8)
+            scales = kept("lb_scales_%d" % g, [P, 2, K_PASS], U8)
+            src = lb_scales_raw[:, :, K_PASS * g : K_PASS * (g + 1)]
             nc.vector.tensor_copy(
-                out=t[:].rearrange("p c (t a m) -> p c a t m", t=PACK, m=16),
-                in_=lbs_raw[:, :, KP * g : KP * (g + 1)].rearrange("p c (a m t) -> p c a t m", t=PACK, m=16),
+                out=scales[:].rearrange("p c (t a m) -> p c a t m", t=SLOTS, m=16),
+                in_=src.rearrange("p c (a m t) -> p c a t m", t=SLOTS, m=16),
             )
-            for c in range(2):
-                for s in range(PACK):
-                    w1_scales[c, g, s] = t[:, c, P * s : P * (s + 1)]
+            for c in zb_passes:
+                for t in range(SLOTS):
+                    weight_scales[c, g, t] = scales[:, c, quarter(t)]
 
         la_sorted = {}
 
-        def sort_la(g):
-            t = kept("la_sorted_%d" % g, [P, PACK * KP], BF16)
-            nc.vector.tensor_copy(
-                out=t[:].rearrange("p (t a m j) -> p a t m j", t=PACK, m=2, j=PACK),
-                in_=la_raw[g][:].rearrange("p j (a m t) -> p a t m j", t=PACK, m=2),
-            )
-            la_sorted[g] = t
+        def la_sort_views(g):
+            la_sorted[g] = kept("la_sorted_%d" % g, [P, SLOTS * K_PASS], BF16)
+            dst = la_sorted[g][:].rearrange("p (t a m r) -> p a t m r", t=SLOTS, m=2, r=SLOTS)
+            src = la_raw[g][:].rearrange("p r (a m t) -> p a t m r", t=SLOTS, m=2)
+            return dst, src
 
-        def quant_la(g):
-            codes = kept("la_codes_%d" % g, [P, KP], U32)
-            scales = kept("la_scales_%d" % g, [P, KP], U8)
+        def quantise_la(g):
+            codes = kept("la_codes_%d" % g, [P, K_PASS], U32)
+            scales = kept("la_scales_%d" % g, [P, K_PASS], U8)
             nc.vector.quantize_mx(out=codes[:].bitcast(FP8X4), scales=scales[:], in_=la_sorted[g][:])
-            for s in range(PACK):
-                w1_codes[2, g, s] = codes[:, P * s : P * (s + 1)].bitcast(FP8X4)
-                w1_scales[2, g, s] = scales[:, P * s : P * (s + 1)]
+            for t in range(SLOTS):
+                weight_codes[ZA_PASS, g, t] = codes[:, quarter(t)].bitcast(FP8X4)
+                weight_scales[ZA_PASS, g, t] = scales[:, quarter(t)]
 
-        z_t = {}
-        z_codes = {}
-        z_scales = {}
+        def sort_zb(mt):
+            ordered = work.tile([P, 2, QUARTERS * PAIRS], F32, name="zb_sorted")
+            nc.vector.tensor_copy(
+                out=ordered[:].rearrange("p u (a i) -> p a u i", i=LINE),
+                in_=zb_words[mt].rearrange("p (a i u) -> p a u i", u=2, i=LINE),
+            )
+            for j in range(QUARTERS):
+                for c in zb_passes:
+                    for u in range(2):
+                        turn_src[mt, c, j, u] = ordered[:, u, quarter(2 * j + c)]
+
+        z_turned = {}
+        z_mx = {}
 
         def turn_z(mt, c, h):
             if h == 0:
-                z_t[mt, c] = work.tile([P, PACK * TILE], BF16, name="z_t", bufs=3, align_bytes=64)
-            words = z_raw[mt, c][:].rearrange("p j k -> p (j k)").bitcast(F32)
+                z_turned[mt, c] = work.tile([P, SLOTS * TILE], BF16, name="z_turned", bufs=PASSES, align_bytes=64)
             ps = bank()
             for jj in range(2):
-                j = 2 * h + jj
                 for u in range(2):
-                    nc.tensor.transpose(
-                        ps[:, P * (2 * jj + u) : P * (2 * jj + u + 1)],
-                        words[:, 256 * j + u : 256 * (j + 1) : 2],
-                        ident[:],
-                    )
+                    nc.tensor.transpose(ps[:, quarter(2 * jj + u)], turn_src[mt, c, 2 * h + jj, u], ident[:])
+            dst = z_turned[mt, c][:].bitcast(F32)[:, TILE * h : TILE * (h + 1)]
             nc.scalar.copy(
-                out=z_t[mt, c][:].bitcast(F32)[:, 512 * h : 512 * (h + 1)].rearrange("p (j r u) -> p j r u", j=2, u=2),
+                out=dst.rearrange("p (j r u) -> p j r u", j=2, u=2),
                 in_=ps[:].rearrange("p (j u r) -> p j r u", j=2, u=2),
             )
 
-        def quant_z(mt, c):
-            z_codes[mt, c] = work.tile([P, TILE], U32, name="z_codes", bufs=6, align_bytes=64)
-            z_scales[mt, c] = work.tile([P, TILE], U8, name="z_scales", bufs=6, align_bytes=64)
-            nc.vector.quantize_mx(out=z_codes[mt, c][:].bitcast(FP8X4), scales=z_scales[mt, c][:], in_=z_t[mt, c][:])
+        def quantise(dst, src, cols):
+            codes, scales = dst
+            nc.vector.quantize_mx(
+                out=codes[:, cols].bitcast(FP8X4),
+                scales=scales[:, cols],
+                in_=src[:, SLOTS * cols.start : SLOTS * cols.stop],
+            )
 
-        def pass1(dst, mt, g, s, c, cols):
+        def quantise_z(mt, c, cols=WHOLE):
+            if cols.start == 0:
+                z_mx[mt, c] = mx_tiles("z", 2 * PASSES)
+            quantise(z_mx[mt, c], z_turned[mt, c], cols)
+
+        def returns_pass(dst, mt, g, t, c, cols):
+            codes, scales = z_mx[mt, c]
             nc.tensor.matmul_mx(
                 out=dst,
-                lhsT=w1_codes[c, g, s],
-                lhsT_scale=w1_scales[c, g, s],
-                rhs=z_codes[mt, c][:, cols].bitcast(FP8X4),
-                rhs_scale=z_scales[mt, c][:, cols],
+                lhsT=weight_codes[c, g, t],
+                lhsT_scale=weight_scales[c, g, t],
+                rhs=codes[:, cols].bitcast(FP8X4),
+                rhs_scale=scales[:, cols],
                 start=(c == 0),
                 stop=(c == PASSES - 1),
             )
 
         growth = {}
 
-        def exp_slot(ps, mt, g, s):
-            if s == 0:
-                growth[mt, g] = work.tile([P, PACK, TILE], F32, name="growth", bufs=2)
-            nc.scalar.activation(out=growth[mt, g][:, s, :], in_=ps[:], func=ACT.Exp)
+        def exp_slot(ps, mt, g, t):
+            if t == 0:
+                growth[mt, g] = work.tile([P, SLOTS, TILE], F32, name="growth")
+            nc.scalar.activation(out=growth[mt, g][:, t, :], in_=ps[:], func=ACT.Exp)
 
-        def returns(mt, g, s):
+        def returns(mt, g, t):
             ps = bank()
             for c in range(PASSES):
-                pass1(ps[:], mt, g, s, c, slice(0, TILE))
-            exp_slot(ps, mt, g, s)
+                returns_pass(ps[:], mt, g, t, c, WHOLE)
+            exp_slot(ps, mt, g, t)
 
         price = {}
-        p_codes = {}
-        p_scales = {}
+        price_mx = {}
 
         def new_price(mt, g):
-            price[mt, g] = work.tile([P, PACK * TILE], BF16, name="price", bufs=2, align_bytes=64)
-            p_codes[mt, g] = work.tile([P, TILE], U32, name="p_codes", bufs=4, align_bytes=64)
-            p_scales[mt, g] = work.tile([P, TILE], U8, name="p_scales", bufs=4, align_bytes=64)
+            price[mt, g] = work.tile([P, SLOTS * TILE], BF16, name="price", align_bytes=64)
+            price_mx[mt, g] = mx_tiles("price", 4)
 
-        def scale_price(mt, g, h):
-            if h == 0:
+        def interleave_views(mt, g, by_slot, cols):
+            if cols.start == 0:
                 new_price(mt, g)
-            half = TILE // 2
-            nc.vector.tensor_tensor(
-                out=price[mt, g][:, PACK * half * h : PACK * half * (h + 1)].rearrange("p (a i t) -> p a t i", i=4, t=PACK),
-                in0=growth[mt, g][:, :, half * h : half * (h + 1)].rearrange("p t (a i) -> p a t i", i=4),
-                in1=fwd[:, g, :].unsqueeze(1).unsqueeze(3).to_broadcast([P, half // 4, PACK, 4]),
-                op=ALU.mult,
+            dst = price[mt, g][:, SLOTS * cols.start : SLOTS * cols.stop]
+            return (
+                dst.rearrange("p (a i t) -> p a t i", i=LINE, t=SLOTS),
+                by_slot[:, :, cols].rearrange("p t (a i) -> p a t i", i=LINE),
             )
 
-        def quant_price(mt, g, cols):
-            nc.vector.quantize_mx(
-                out=p_codes[mt, g][:, cols].bitcast(FP8X4),
-                scales=p_scales[mt, g][:, cols],
-                in_=price[mt, g][:, PACK * cols.start : PACK * cols.stop],
-            )
+        def make_price(mt, g, cols):
+            dst, src = interleave_views(mt, g, growth[mt, g], cols)
+            factor = fwd[:, g, :].unsqueeze(1).unsqueeze(3).to_broadcast(list(dst.shape))
+            nc.vector.tensor_tensor(out=dst, in0=src, in1=factor, op=ALU.mult)
 
-        def quant_price_halves(mt, g):
-            for h in range(2):
-                quant_price(mt, g, slice(256 * h, 256 * (h + 1)))
+        def quantise_price(mt, g, cols):
+            quantise(price_mx[mt, g], price[mt, g], cols)
 
         def baskets(mt, j):
             ps = bank()
-            cols = slice(P * j, P * (j + 1))
             for g in range(2):
+                codes, scales = price_mx[mt, g]
                 nc.tensor.matmul_mx(
                     out=ps[:],
-                    lhsT=p_codes[mt, g][:, cols].bitcast(FP8X4),
-                    lhsT_scale=p_scales[mt, g][:, cols],
-                    rhs=ww[:, g, :].bitcast(FP4X4),
-                    rhs_scale=ws[:, g, :],
+                    lhsT=codes[:, quarter(j)].bitcast(FP8X4),
+                    lhsT_scale=scales[:, quarter(j)],
+                    rhs=w_codes[:, g, :].bitcast(FP4X4),
+                    rhs_scale=w_scales_sb[:, g, :],
                     start=(g == 0),
                     stop=(g == 1),
                 )
-            gain = work.tile([P, B], F32, name="gain", bufs=3)
-            nc.vector.tensor_tensor(out=gain[:], in0=ps[:], in1=strike_b[:], op=ALU.subtract)
-            payoff = work.tile([P, B], F32, name="payoff", bufs=4)
+            gain = work.tile([P, B], F32, name="gain", bufs=QUARTERS)
+            payoff = work.tile([P, B], F32, name="payoff", bufs=QUARTERS)
+            nc.vector.tensor_tensor(out=gain[:], in0=ps[:], in1=strike_rows[:], op=ALU.subtract)
             nc.scalar.activation(out=payoff[:], in_=gain[:], func=ACT.Relu)
-            rows = out[TILE * mt : TILE * (mt + 1), :].rearrange("(p j) b -> p j b", j=PACK)
+            rows = out[TILE * mt : TILE * (mt + 1), :].rearrange("(p j) b -> p j b", j=QUARTERS)
             nc.sync.dma_start(out=rows[:, j, :], in_=payoff[:])
 
-        grown = {}
-
-        def narrow_returns(mt, g, j):
-            ps = bank()
-            cols = slice(P * j, P * (j + 1))
-            for s in range(PACK):
-                for c in range(PASSES):
-                    pass1(ps[:, P * s : P * (s + 1)], mt, g, s, c, cols)
-            grown[j] = work.tile([P, P, PACK], F32, name="grown", bufs=4)
-            nc.scalar.activation(out=grown[j][:], in_=ps[:].rearrange("p (t n) -> p n t", t=PACK), func=ACT.Exp)
-
-        def narrow_price(mt, g, j):
-            nc.vector.tensor_tensor(
-                out=price[mt, g][:, PACK * P * j : PACK * P * (j + 1)].rearrange("p (n t) -> p n t", t=PACK),
-                in0=grown[j][:],
-                in1=fwd[:, g, :].unsqueeze(1).to_broadcast([P, P, PACK]),
-                op=ALU.mult,
-            )
-
-        whole = slice(0, TILE)
         sort_lb_codes(0, 0)
         sort_lb_scales(0)
-        sort_lb_codes(1, 0)
-        for c in range(2):
-            for h in range(2):
-                turn_z(0, c, h)
-        quant_z(0, 0)
-        first = [bank() for s in range(PACK)]
-        for s in range(PACK):
-            pass1(first[s][:], 0, 0, s, 0, whole)
-        sort_la(0)
-        quant_z(0, 1)
-        quant_la(0)
-        for h in range(2):
-            turn_z(0, 2, h)
-        quant_z(0, 2)
-        for s in range(PACK):
-            pass1(first[s][:], 0, 0, s, 1, whole)
-        for s in range(PACK):
-            pass1(first[s][:], 0, 0, s, 2, whole)
-            exp_slot(first[s], 0, 0, s)
-        sort_lb_codes(0, 1)
+        turn_z(0, 0, 0)
+        turn_z(0, 1, 0)
+        quantise_z(0, 0, HALVES[0])
         sort_lb_scales(1)
+        turn_z(0, 0, 1)
+        turn_z(0, 1, 1)
+        sort_lb_codes(1, 0)
+        quantise_z(0, 0, HALVES[1])
+        for h in range(2):
+            turn_z(0, ZA_PASS, h)
+        open_banks = [bank() for t in range(SLOTS)]
+        for t in range(SLOTS):
+            returns_pass(open_banks[t][:], 0, 0, t, 0, WHOLE)
+        quantise_z(0, 1)
+        for t in range(SLOTS):
+            returns_pass(open_banks[t][:], 0, 0, t, 1, WHOLE)
+        dst, src = la_sort_views(0)
+        nc.scalar.copy(out=dst[:, :LA_BLOCKS_ON_SCALAR], in_=src[:, :LA_BLOCKS_ON_SCALAR])
+        nc.vector.tensor_copy(out=dst[:, LA_BLOCKS_ON_SCALAR:], in_=src[:, LA_BLOCKS_ON_SCALAR:])
+        quantise_z(0, ZA_PASS)
+        quantise_la(0)
+        dst, src = la_sort_views(1)
+        nc.vector.tensor_copy(out=dst, in_=src)
+        for t in range(SLOTS):
+            returns_pass(open_banks[t][:], 0, 0, t, ZA_PASS, WHOLE)
+            exp_slot(open_banks[t], 0, 0, t)
+        sort_lb_codes(0, 1)
         sort_lb_codes(1, 1)
-        sort_la(1)
-        quant_la(1)
+        fwd32 = kept("fwd32", [P, 2, SLOTS], F32)
+        nc.vector.tensor_copy(out=fwd32[:], in_=fwd[:])
+        quantise_la(1)
 
         for mt in range(TILES - 1):
-            if mt > 0:
-                for s in range(PACK):
-                    returns(mt, 0, s)
-            for c, h in ((0, 0), (0, 1), (1, 0)):
-                turn_z(mt + 1, c, h)
-            scale_price(mt, 0, 0)
-            quant_z(mt + 1, 0)
-            if mt > 0:
-                for j in range(PACK):
-                    baskets(mt - 1, j)
+            if mt == 0:
+                turns = [(c, h) for h in range(2) for c in zb_passes]
+                first_run = FIRST_RUN_TILE_1
             else:
-                for s in range(2):
-                    returns(mt, 1, s)
-            scale_price(mt, 0, 1)
-            quant_price_halves(mt, 0)
-            for c, h in ((1, 1), (2, 0), (2, 1)):
+                turns = [(c, h) for c in zb_passes for h in range(2)]
+                first_run = FIRST_RUN
+                for t in range(SLOTS):
+                    returns(mt, 0, t)
+            turns += [(ZA_PASS, h) for h in range(2)]
+            for c, h in turns[:first_run]:
                 turn_z(mt + 1, c, h)
-            quant_z(mt + 1, 1)
-            quant_z(mt + 1, 2)
-            for s in range(0 if mt > 0 else 2, PACK):
-                returns(mt, 1, s)
-            for h in range(2):
-                scale_price(mt, 1, h)
-            quant_price_halves(mt, 1)
+            make_price(mt, 0, HALVES[0])
+            quantise_z(mt + 1, 0)
+            if mt == 0:
+                slots_left = range(2, SLOTS)
+                for t in range(2):
+                    returns(mt, 1, t)
+            else:
+                slots_left = range(SLOTS)
+                for j in range(QUARTERS):
+                    baskets(mt - 1, j)
+            make_price(mt, 0, HALVES[1])
+            for cols in HALVES:
+                quantise_price(mt, 0, cols)
+            for c, h in turns[first_run:]:
+                turn_z(mt + 1, c, h)
+            quantise_z(mt + 1, 1)
+            quantise_z(mt + 1, ZA_PASS)
+            if mt + 2 < TILES:
+                sort_zb(mt + 2)
+            for t in slots_left:
+                returns(mt, 1, t)
+            pieces = HALVES if mt + 2 < TILES else QUARTER_COLS
+            for step in range(len(pieces) + 1):
+                if step < len(pieces):
+                    make_price(mt, 1, pieces[step])
+                if step > 0:
+                    quantise_price(mt, 1, pieces[step - 1])
 
         mt = TILES - 1
-        for s in range(PACK):
-            returns(mt, 0, s)
-        narrow_returns(mt, 1, 0)
-        scale_price(mt, 0, 0)
-        for j in range(PACK):
+        rounded = kept("rounded", [P, SLOTS, TILE], BF16)
+        for step in range(SLOTS + 1):
+            if step < SLOTS:
+                returns(mt, 0, step)
+            if step > 0:
+                t = step - 1
+                nc.scalar.activation(
+                    out=rounded[:, t, :], in_=growth[mt, 0][:, t, :], func=ACT.Copy, scale=fwd32[:, 0, t : t + 1]
+                )
+        for j in range(QUARTERS):
             baskets(mt - 1, j)
-        for j in range(1, PACK):
-            narrow_returns(mt, 1, j)
-        scale_price(mt, 0, 1)
-        quant_price_halves(mt, 0)
+
+        last_growth = kept("last_growth", [P, TILE, SLOTS], F32)
+        for cols in QUARTER_COLS:
+            ps = bank()
+            for t in range(SLOTS):
+                for c in range(PASSES):
+                    returns_pass(ps[:, quarter(t)], mt, 1, t, c, cols)
+            nc.scalar.activation(
+                out=last_growth[:, cols, :], in_=ps[:].rearrange("p (t n) -> p n t", t=SLOTS), func=ACT.Exp
+            )
+        for cols in HALVES:
+            dst, src = interleave_views(mt, 0, rounded, cols)
+            nc.vector.tensor_copy(out=dst, in_=src)
+        for cols in HALVES:
+            quantise_price(mt, 0, cols)
         new_price(mt, 1)
-        for step in range(PACK + 2):
-            if step < PACK:
-                narrow_price(mt, 1, step)
-            if 1 <= step <= PACK:
-                quant_price(mt, 1, slice(P * (step - 1), P * step))
+        last_price = price[mt, 1][:].rearrange("p (n t) -> p n t", t=SLOTS)
+        factor = fwd[:, 1, :].unsqueeze(1).to_broadcast([P, P, SLOTS])
+        for step in range(QUARTERS + 2):
+            if step < QUARTERS:
+                cols = quarter(step)
+                nc.vector.tensor_tensor(out=last_price[:, cols, :], in0=last_growth[:, cols, :], in1=factor, op=ALU.mult)
+            if 1 <= step <= QUARTERS:
+                quantise_price(mt, 1, quarter(step - 1))
             if step >= 2:
                 baskets(mt, step - 2)

from contextlib import ExitStack

import concourse.mybir as mybir
from concourse.masks import make_identity

M, KA, KB, N, B = 2048, 512, 1024, 1024, 512
FLOPS = 2 * M * (KA + KB) * N + 2 * M * N * B

F32 = mybir.dt.float32
BF16 = mybir.dt.bfloat16
U32 = mybir.dt.uint32
I32 = mybir.dt.int32
U8 = mybir.dt.uint8
FP8X4 = mybir.dt.float8_e4m3fn_x4
FP4X4 = mybir.dt.float4_e2m1fn_x4
ACT = mybir.ActivationFunctionType
ALU = mybir.AluOpType

P = 128
SLOTS = 4
K_PASS = P * SLOTS
PAIRS = K_PASS // 2
TILE = 512
QUARTERS = TILE // P
TILES = M // TILE
PASSES = (KB + KA) // K_PASS
ZA_PASS = PASSES - 1
LINE = 4

LA_BLOCKS_ON_SCALAR = 16
FIRST_RUN_TILE_1 = 3
FIRST_RUN = 4

WHOLE = slice(0, TILE)
HALVES = (slice(0, TILE // 2), slice(TILE // 2, TILE))
QUARTER_COLS = tuple(slice(P * j, P * (j + 1)) for j in range(QUARTERS))


def quarter(j):
    return slice(P * j, P * (j + 1))


def tile_basket_option_payoff_s3_kernel(
    tc, za, zb, la, lb_words, lb_scales, forward, w_words, w_scales, strike, out
):
    nc = tc.nc
    with ExitStack() as ctx:
        keep = ctx.enter_context(tc.tile_pool(name="keep", bufs=1))
        work = ctx.enter_context(tc.tile_pool(name="work", bufs=2))
        psum = ctx.enter_context(tc.psum_pool(name="psum", bufs=8))
        ctx.enter_context(tc.manual_schedule())

        def kept(name, shape, dtype):
            return keep.tile(shape, dtype, name=name, align_bytes=64)

        def bank():
            return psum.tile([P, TILE], F32, name="bank")

        def mx_tiles(name, bufs):
            codes = work.tile([P, TILE], U32, name=name + "_codes", bufs=bufs, align_bytes=64)
            scales = work.tile([P, TILE], U8, name=name + "_scales", bufs=bufs, align_bytes=64)
            return codes, scales

        ident = kept("ident", [P, P], F32)
        make_identity(nc, ident[:])

        lb_scales_raw = kept("lb_scales_raw", [P, 2, N], U8)
        w_scales_sb = kept("w_scales_sb", [P, 2, B], U8)
        nc.vector.memset(lb_scales_raw[:].bitcast(I32), 0)
        nc.vector.memset(w_scales_sb[:].bitcast(I32), 0)

        def load_scales(queue, dst, src):
            for q in range(4):
                queue.dma_start(
                    out=dst[32 * q : 32 * q + 4, :, :].bitcast(I32),
                    in_=src[:, 4 * q : 4 * q + 4, :].rearrange("c r n -> r c n").bitcast(I32),
                )

        turn_src = {}
        zb_words = {}

        def load_z(mt, src, passes, part, parts):
            width = src.shape[1]
            rows = src[TILE * mt : TILE * (mt + 1), :].rearrange("(p j) k -> p j k", j=QUARTERS)
            count = QUARTERS // parts
            raw = kept("z_raw_%d_%d_%d" % (mt, passes[0], part), [P, count, width], BF16)
            nc.sync.dma_start(out=raw[:], in_=rows[:, count * part : count * (part + 1), :])
            words = raw[:].rearrange("p j k -> p (j k)").bitcast(F32)
            for j in range(count):
                for i, c in enumerate(passes):
                    at = (width // 2) * j + PAIRS * i
                    for u in range(2):
                        turn_src[mt, c, count * part + j, u] = words[:, at + u : at + PAIRS : 2]
            return words

        lb_raw = {}

        def load_lb(c, g):
            lb_raw[c, g] = kept("lb_raw_%d_%d" % (c, g), [P, 2 * K_PASS], U8)
            src = lb_words[c, :, 2 * K_PASS * g : 2 * K_PASS * (g + 1)]
            nc.sync.dma_start(out=lb_raw[c, g][:].bitcast(I32), in_=src.bitcast(I32))

        la_raw = {}

        def load_la(g):
            la_raw[g] = kept("la_raw_%d" % g, [P, SLOTS, K_PASS], BF16)
            src = la[:, K_PASS * g : K_PASS * (g + 1)].rearrange("(p t) n -> p t n", t=SLOTS)
            nc.sync.dma_start(out=la_raw[g][:], in_=src)

        zb_passes = (0, 1)
        load_z(0, zb, zb_passes, 0, 2)
        load_lb(0, 0)
        load_scales(nc.scalar, lb_scales_raw, lb_scales)
        load_z(0, zb, zb_passes, 1, 2)
        load_lb(1, 0)
        load_z(0, za, (ZA_PASS,), 0, 1)
        load_la(0)
        load_lb(0, 1)
        load_lb(1, 1)
        load_la(1)
        fwd = kept("fwd", [P, 2, SLOTS], BF16)
        nc.sync.dma_start(out=fwd[:], in_=forward.rearrange("(g p t) -> p g t", p=P, t=SLOTS))
        for part in range(2):
            load_z(1, zb, zb_passes, part, 2)
        load_z(1, za, (ZA_PASS,), 0, 1)
        load_scales(nc.sync, w_scales_sb, w_scales)
        w_codes = kept("w_codes", [P, 2, 2 * B], U8)
        nc.sync.dma_start(out=w_codes[:].bitcast(I32), in_=w_words.rearrange("g p n -> p g n").bitcast(I32))
        strike_rows = kept("strike_rows", [P, B], BF16)
        nc.sync.dma_start(out=strike_rows[:], in_=strike.partition_broadcast(P))
        for mt in range(2, TILES):
            zb_words[mt] = load_z(mt, zb, zb_passes, 0, 1)
            load_z(mt, za, (ZA_PASS,), 0, 1)

        weight_codes = {}
        weight_scales = {}

        def sort_lb_codes(c, g):
            codes = kept("lb_codes_%d_%d" % (c, g), [P, 2 * K_PASS], U8)
            nc.vector.tensor_copy(
                out=codes[:].rearrange("p (t a m b) -> p a t m b", t=SLOTS, m=8, b=2),
                in_=lb_raw[c, g][:].rearrange("p (a m t b) -> p a t m b", t=SLOTS, m=8, b=2),
            )
            for t in range(SLOTS):
                weight_codes[c, g, t] = codes[:, 2 * P * t : 2 * P * (t + 1)].bitcast(FP4X4)

        def sort_lb_scales(g):
            scales = kept("lb_scales_%d" % g, [P, 2, K_PASS], U8)
            src = lb_scales_raw[:, :, K_PASS * g : K_PASS * (g + 1)]
            nc.vector.tensor_copy(
                out=scales[:].rearrange("p c (t a m) -> p c a t m", t=SLOTS, m=16),
                in_=src.rearrange("p c (a m t) -> p c a t m", t=SLOTS, m=16),
            )
            for c in zb_passes:
                for t in range(SLOTS):
                    weight_scales[c, g, t] = scales[:, c, quarter(t)]

        la_sorted = {}

        def la_sort_views(g):
            la_sorted[g] = kept("la_sorted_%d" % g, [P, SLOTS * K_PASS], BF16)
            dst = la_sorted[g][:].rearrange("p (t a m r) -> p a t m r", t=SLOTS, m=2, r=SLOTS)
            src = la_raw[g][:].rearrange("p r (a m t) -> p a t m r", t=SLOTS, m=2)
            return dst, src

        def quantise_la(g):
            codes = kept("la_codes_%d" % g, [P, K_PASS], U32)
            scales = kept("la_scales_%d" % g, [P, K_PASS], U8)
            nc.vector.quantize_mx(out=codes[:].bitcast(FP8X4), scales=scales[:], in_=la_sorted[g][:])
            for t in range(SLOTS):
                weight_codes[ZA_PASS, g, t] = codes[:, quarter(t)].bitcast(FP8X4)
                weight_scales[ZA_PASS, g, t] = scales[:, quarter(t)]

        def sort_zb(mt):
            ordered = work.tile([P, 2, QUARTERS * PAIRS], F32, name="zb_sorted")
            nc.vector.tensor_copy(
                out=ordered[:].rearrange("p u (a i) -> p a u i", i=LINE),
                in_=zb_words[mt].rearrange("p (a i u) -> p a u i", u=2, i=LINE),
            )
            for j in range(QUARTERS):
                for c in zb_passes:
                    for u in range(2):
                        turn_src[mt, c, j, u] = ordered[:, u, quarter(2 * j + c)]

        z_turned = {}
        z_mx = {}

        def turn_z(mt, c, h):
            if h == 0:
                z_turned[mt, c] = work.tile([P, SLOTS * TILE], BF16, name="z_turned", bufs=PASSES, align_bytes=64)
            ps = bank()
            for jj in range(2):
                for u in range(2):
                    nc.tensor.transpose(ps[:, quarter(2 * jj + u)], turn_src[mt, c, 2 * h + jj, u], ident[:])
            dst = z_turned[mt, c][:].bitcast(F32)[:, TILE * h : TILE * (h + 1)]
            nc.scalar.copy(
                out=dst.rearrange("p (j r u) -> p j r u", j=2, u=2),
                in_=ps[:].rearrange("p (j u r) -> p j r u", j=2, u=2),
            )

        def quantise(dst, src, cols):
            codes, scales = dst
            nc.vector.quantize_mx(
                out=codes[:, cols].bitcast(FP8X4),
                scales=scales[:, cols],
                in_=src[:, SLOTS * cols.start : SLOTS * cols.stop],
            )

        def quantise_z(mt, c, cols=WHOLE):
            if cols.start == 0:
                z_mx[mt, c] = mx_tiles("z", 2 * PASSES)
            quantise(z_mx[mt, c], z_turned[mt, c], cols)

        def returns_pass(dst, mt, g, t, c, cols):
            codes, scales = z_mx[mt, c]
            nc.tensor.matmul_mx(
                out=dst,
                lhsT=weight_codes[c, g, t],
                lhsT_scale=weight_scales[c, g, t],
                rhs=codes[:, cols].bitcast(FP8X4),
                rhs_scale=scales[:, cols],
                start=(c == 0),
                stop=(c == PASSES - 1),
            )

        growth = {}

        def exp_slot(ps, mt, g, t):
            if t == 0:
                growth[mt, g] = work.tile([P, SLOTS, TILE], F32, name="growth")
            nc.scalar.activation(out=growth[mt, g][:, t, :], in_=ps[:], func=ACT.Exp)

        def returns(mt, g, t):
            ps = bank()
            for c in range(PASSES):
                returns_pass(ps[:], mt, g, t, c, WHOLE)
            exp_slot(ps, mt, g, t)

        price = {}
        price_mx = {}

        def new_price(mt, g):
            price[mt, g] = work.tile([P, SLOTS * TILE], BF16, name="price", align_bytes=64)
            price_mx[mt, g] = mx_tiles("price", 4)

        def interleave_views(mt, g, by_slot, cols):
            if cols.start == 0:
                new_price(mt, g)
            dst = price[mt, g][:, SLOTS * cols.start : SLOTS * cols.stop]
            return (
                dst.rearrange("p (a i t) -> p a t i", i=LINE, t=SLOTS),
                by_slot[:, :, cols].rearrange("p t (a i) -> p a t i", i=LINE),
            )

        def make_price(mt, g, cols):
            dst, src = interleave_views(mt, g, growth[mt, g], cols)
            factor = fwd[:, g, :].unsqueeze(1).unsqueeze(3).to_broadcast(list(dst.shape))
            nc.vector.tensor_tensor(out=dst, in0=src, in1=factor, op=ALU.mult)

        def quantise_price(mt, g, cols):
            quantise(price_mx[mt, g], price[mt, g], cols)

        def baskets(mt, j):
            ps = bank()
            for g in range(2):
                codes, scales = price_mx[mt, g]
                nc.tensor.matmul_mx(
                    out=ps[:],
                    lhsT=codes[:, quarter(j)].bitcast(FP8X4),
                    lhsT_scale=scales[:, quarter(j)],
                    rhs=w_codes[:, g, :].bitcast(FP4X4),
                    rhs_scale=w_scales_sb[:, g, :],
                    start=(g == 0),
                    stop=(g == 1),
                )
            gain = work.tile([P, B], F32, name="gain", bufs=QUARTERS)
            payoff = work.tile([P, B], F32, name="payoff", bufs=QUARTERS)
            nc.vector.tensor_tensor(out=gain[:], in0=ps[:], in1=strike_rows[:], op=ALU.subtract)
            nc.scalar.activation(out=payoff[:], in_=gain[:], func=ACT.Relu)
            rows = out[TILE * mt : TILE * (mt + 1), :].rearrange("(p j) b -> p j b", j=QUARTERS)
            nc.sync.dma_start(out=rows[:, j, :], in_=payoff[:])

        sort_lb_codes(0, 0)
        sort_lb_scales(0)
        turn_z(0, 0, 0)
        turn_z(0, 1, 0)
        quantise_z(0, 0, HALVES[0])
        sort_lb_scales(1)
        turn_z(0, 0, 1)
        turn_z(0, 1, 1)
        sort_lb_codes(1, 0)
        quantise_z(0, 0, HALVES[1])
        for h in range(2):
            turn_z(0, ZA_PASS, h)
        open_banks = [bank() for t in range(SLOTS)]
        for t in range(SLOTS):
            returns_pass(open_banks[t][:], 0, 0, t, 0, WHOLE)
        quantise_z(0, 1)
        for t in range(SLOTS):
            returns_pass(open_banks[t][:], 0, 0, t, 1, WHOLE)
        dst, src = la_sort_views(0)
        nc.scalar.copy(out=dst[:, :LA_BLOCKS_ON_SCALAR], in_=src[:, :LA_BLOCKS_ON_SCALAR])
        nc.vector.tensor_copy(out=dst[:, LA_BLOCKS_ON_SCALAR:], in_=src[:, LA_BLOCKS_ON_SCALAR:])
        quantise_z(0, ZA_PASS)
        quantise_la(0)
        dst, src = la_sort_views(1)
        nc.vector.tensor_copy(out=dst, in_=src)
        for t in range(SLOTS):
            returns_pass(open_banks[t][:], 0, 0, t, ZA_PASS, WHOLE)
            exp_slot(open_banks[t], 0, 0, t)
        sort_lb_codes(0, 1)
        sort_lb_codes(1, 1)
        fwd32 = kept("fwd32", [P, 2, SLOTS], F32)
        nc.vector.tensor_copy(out=fwd32[:], in_=fwd[:])
        quantise_la(1)

        for mt in range(TILES - 1):
            if mt == 0:
                turns = [(c, h) for h in range(2) for c in zb_passes]
                first_run = FIRST_RUN_TILE_1
            else:
                turns = [(c, h) for c in zb_passes for h in range(2)]
                first_run = FIRST_RUN
                for t in range(SLOTS):
                    returns(mt, 0, t)
            turns += [(ZA_PASS, h) for h in range(2)]
            for c, h in turns[:first_run]:
                turn_z(mt + 1, c, h)
            make_price(mt, 0, HALVES[0])
            quantise_z(mt + 1, 0)
            if mt == 0:
                slots_left = range(2, SLOTS)
                for t in range(2):
                    returns(mt, 1, t)
            else:
                slots_left = range(SLOTS)
                for j in range(QUARTERS):
                    baskets(mt - 1, j)
            make_price(mt, 0, HALVES[1])
            for cols in HALVES:
                quantise_price(mt, 0, cols)
            for c, h in turns[first_run:]:
                turn_z(mt + 1, c, h)
            quantise_z(mt + 1, 1)
            quantise_z(mt + 1, ZA_PASS)
            if mt + 2 < TILES:
                sort_zb(mt + 2)
            for t in slots_left:
                returns(mt, 1, t)
            pieces = HALVES if mt + 2 < TILES else QUARTER_COLS
            for step in range(len(pieces) + 1):
                if step < len(pieces):
                    make_price(mt, 1, pieces[step])
                if step > 0:
                    quantise_price(mt, 1, pieces[step - 1])

        mt = TILES - 1
        rounded = kept("rounded", [P, SLOTS, TILE], BF16)
        for step in range(SLOTS + 1):
            if step < SLOTS:
                returns(mt, 0, step)
            if step > 0:
                t = step - 1
                nc.scalar.activation(
                    out=rounded[:, t, :], in_=growth[mt, 0][:, t, :], func=ACT.Copy, scale=fwd32[:, 0, t : t + 1]
                )
        for j in range(QUARTERS):
            baskets(mt - 1, j)

        last_growth = kept("last_growth", [P, TILE, SLOTS], F32)
        for cols in QUARTER_COLS:
            ps = bank()
            for t in range(SLOTS):
                for c in range(PASSES):
                    returns_pass(ps[:, quarter(t)], mt, 1, t, c, cols)
            nc.scalar.activation(
                out=last_growth[:, cols, :], in_=ps[:].rearrange("p (t n) -> p n t", t=SLOTS), func=ACT.Exp
            )
        for cols in HALVES:
            dst, src = interleave_views(mt, 0, rounded, cols)
            nc.vector.tensor_copy(out=dst, in_=src)
        for cols in HALVES:
            quantise_price(mt, 0, cols)
        new_price(mt, 1)
        last_price = price[mt, 1][:].rearrange("p (n t) -> p n t", t=SLOTS)
        factor = fwd[:, 1, :].unsqueeze(1).to_broadcast([P, P, SLOTS])
        for step in range(QUARTERS + 2):
            if step < QUARTERS:
                cols = quarter(step)
                nc.vector.tensor_tensor(out=last_price[:, cols, :], in0=last_growth[:, cols, :], in1=factor, op=ALU.mult)
            if 1 <= step <= QUARTERS:
                quantise_price(mt, 1, quarter(step - 1))
            if step >= 2:
                baskets(mt, step - 2)
